import numpy as np, ml_dtypes
CORES = [45,53,77,117,47,55,79,119]
N = 8
TOK, K, FT = 32, 3, 2
ROUTE = [[[0,4,6],[5,6,7],[4,5,7],[2,3,5],[5,6,7],[2,4,7],[1,3,7],[0,1,6],[1,2,7],[0,3,6],[1,2,4],[1,4,6],[4,5,6],[0,2,4],[1,3,6],[5,6,7],[5,6,7],[0,1,6],[0,2,7],[0,1,3],[0,4,6],[3,5,7],[0,3,6],[0,4,7],[1,2,6],[2,5,6],[1,5,7],[0,1,2],[0,2,5],[0,3,7],[0,1,4],[5,6,7]],[[0,2,3],[0,4,7],[2,4,7],[0,1,3],[0,2,3],[0,4,7],[0,3,4],[1,4,7],[3,4,6],[0,1,5],[2,3,4],[2,5,6],[2,6,7],[0,1,7],[1,5,6],[0,4,5],[0,1,3],[1,6,7],[0,3,4],[1,4,7],[2,3,6],[1,2,4],[0,2,7],[0,1,3],[2,4,7],[4,6,7],[2,3,5],[2,4,5],[0,2,4],[0,1,3],[0,4,5],[1,6,7]],[[0,3,6],[1,2,3],[1,2,6],[1,3,5],[0,2,4],[2,3,4],[1,2,7],[0,1,4],[4,5,6],[0,1,4],[0,5,6],[2,4,7],[0,2,7],[0,1,7],[1,5,6],[3,4,5],[0,4,6],[2,5,7],[0,1,3],[0,3,7],[4,5,7],[0,1,5],[4,5,6],[0,4,5],[0,1,4],[0,5,6],[2,5,6],[0,5,6],[5,6,7],[0,3,6],[0,5,7],[2,4,6]],[[2,4,7],[1,2,3],[1,3,4],[3,5,6],[1,4,7],[3,4,6],[1,4,5],[0,2,4],[0,1,7],[0,1,2],[1,4,5],[0,2,7],[1,5,7],[4,5,6],[0,3,6],[3,5,7],[1,2,6],[0,4,6],[2,4,5],[0,1,7],[1,2,6],[0,2,3],[1,2,7],[3,4,7],[1,2,7],[0,2,6],[1,3,6],[2,4,7],[4,5,6],[1,2,5],[0,5,7],[1,2,7]],[[0,4,5],[4,5,6],[2,6,7],[1,3,6],[0,3,4],[0,3,5],[0,3,6],[2,4,7],[0,2,7],[3,4,7],[0,2,3],[2,3,4],[0,3,5],[1,4,6],[2,3,5],[3,6,7],[4,6,7],[3,6,7],[3,4,7],[0,3,6],[2,5,6],[4,6,7],[0,1,3],[0,1,5],[5,6,7],[3,6,7],[0,3,7],[0,2,7],[2,4,6],[1,2,4],[1,3,6],[1,2,5]],[[1,3,6],[0,4,5],[1,4,7],[3,4,6],[2,3,4],[3,5,7],[2,4,7],[2,3,7],[0,5,7],[2,4,6],[1,2,4],[1,3,5],[1,3,6],[1,3,7],[3,5,7],[2,4,7],[0,6,7],[1,3,7],[1,3,4],[0,1,7],[2,3,7],[2,4,7],[0,2,6],[0,4,7],[1,2,5],[1,4,5],[0,1,7],[0,6,7],[2,4,6],[0,4,5],[2,3,5],[0,4,5]],[[2,3,7],[1,2,7],[2,4,6],[0,2,4],[2,3,7],[3,5,6],[0,5,6],[3,4,6],[2,3,5],[2,4,5],[1,3,7],[0,2,6],[0,2,7],[2,4,6],[2,4,7],[1,3,4],[0,3,4],[0,3,4],[0,1,4],[5,6,7],[2,5,7],[0,3,6],[3,5,6],[1,3,5],[0,4,6],[2,3,6],[0,5,6],[0,2,7],[0,1,5],[2,5,7],[4,5,6],[0,2,5]],[[0,1,5],[0,4,5],[0,5,6],[0,3,7],[0,3,7],[1,6,7],[1,3,5],[2,3,5],[0,1,4],[3,4,7],[0,1,6],[0,4,6],[2,5,6],[1,3,7],[0,2,6],[1,3,4],[5,6,7],[2,3,6],[2,4,6],[1,2,3],[2,5,6],[1,2,4],[2,3,7],[0,3,6],[1,3,7],[0,1,7],[2,4,7],[5,6,7],[0,4,6],[0,2,6],[0,2,7],[0,3,7]]]
def setup_inputs(rng):
    return {"x": rng.standard_normal((N, 128, TOK), dtype=np.float32).astype(ml_dtypes.bfloat16), "gate": (0.5 * rng.integers(1, 4, size=(N, K, TOK)) * (2 * rng.integers(0, 2, size=(N, K, TOK)) - 1)).astype(np.float32).astype(ml_dtypes.bfloat16), "w1": (rng.standard_normal((N, 128, FT * 128), dtype=np.float32) / 8).astype(ml_dtypes.bfloat16), "w2": (rng.standard_normal((N, 128, FT * 128), dtype=np.float32) / 8).astype(ml_dtypes.bfloat16)}
def setup_inputs_big(rng):
    d = setup_inputs(rng)
    for k in ("x", "gate", "w1", "w2"): d[k] = (d[k].astype(np.float32) * 1024.0).astype(d[k].dtype)
    return d
def setup_inputs_small(rng):
    d = setup_inputs(rng)
    for k in ("x", "gate", "w1", "w2"): d[k] = (d[k].astype(np.float32) * (1 / 1024.0)).astype(d[k].dtype)
    return d
def reference(x, gate, w1, w2):
    X, GATE, W1, W2 = x.astype(np.float64), gate.astype(np.float64), w1.astype(np.float64), w2.astype(np.float64)
    y = np.zeros((N, 128, TOK))
    for r in range(N):
        for t in range(TOK):
            for i, e in enumerate(ROUTE[r][t]):
                hid = np.maximum(W1[e].T @ X[r][:, t], 0.0)
                y[r][:, t] += GATE[r][i, t] * sum(W2[e][:, 128 * f:128 * f + 128].T @ hid[128 * f:128 * f + 128] for f in range(FT))
    return {"y": y.astype(ml_dtypes.bfloat16)}

@@ -1,0 +1,282 @@
+from concourse.bass import DstId, RemoteDMATransfer
+from concourse.mybir import AluOpType
+
+NRANK = 8
+NROUND = 4
+TOK = 32
+BLK = 2 * TOK
+
+SCRATCH = {
+    "xo": ("sbuf", [128, TOK], "bfloat16"),
+    "xr": ("sbuf", [128, TOK], "bfloat16"),
+    "xu": ("sbuf", [128, NRANK * TOK], "bfloat16"),
+    "wo": ("sbuf", [128, 512], "bfloat16"),
+    "wp": ("sbuf", [128, 512], "bfloat16"),
+    "zero": ("sbuf", [128, 128], "float32"),
+    "ones": ("sbuf", [128, 128], "bfloat16"),
+    "g1": ("sbuf", [128, 96], "bfloat16"),
+    "hs": ("sbuf", [128, NROUND * 128], "bfloat16"),
+    "ro": ("sbuf", [128, NROUND * BLK], "bfloat16"),
+    "land": ("sbuf", [128, 4 * BLK], "bfloat16"),
+    "pr": ("sbuf", [128, 4 * BLK], "float32"),
+    "s3": ("sbuf", [128, BLK], "float32"),
+    "yo": ("sbuf", [128, TOK], "bfloat16"),
+    "gd": ("psum", [128, 512], "float32"),
+    "pb0": ("psum", [128, 512], "float32"),
+    "pb1": ("psum", [128, 512], "float32"),
+    "pb2": ("psum", [128, 512], "float32"),
+    "pb3": ("psum", [128, 512], "float32"),
+}
+SEMAPHORES = (["ldx", "ldw", "ldg", "fill", "gsc", "xrs", "wps", "sent", "cmb", "yv", "stored"]
+              + ["xs%d" % r for r in range(NRANK)] + ["ret%d" % j for j in range(4)]
+              + ["%s%d" % (s, n) for s in ("hh", "rl", "rr", "cp") for n in range(NROUND)])
+
+
+def _bits(mask):
+    return [k for k in range(16) if (mask >> k) & 1]
+
+
+def _nbits(mask):
+    return len(_bits(mask))
+
+
+def make_plan(cores, topo):
+    chips = sorted(set(topo.chip(c) for c in cores))
+    reach = lambda c: sum(1 for d in cores if d != c and topo.may_write(c, d))
+    members = {ch: sorted([c for c in cores if topo.chip(c) == ch], key=lambda c: (reach(c), c)) for ch in chips}
+    planes = []
+    for ch in chips:
+        for grp in planes:
+            if topo.same_plane(grp[0], ch):
+                grp.append(ch)
+                break
+        else:
+            planes.append([ch])
+    where = {ch: (gi, grp.index(ch)) for gi, grp in enumerate(planes) for ch in grp}
+
+    def step(src_chip, dst_chip):
+        return (where[dst_chip][1] - where[src_chip][1]) % len(planes[where[dst_chip][0]])
+
+    def blk(rcv_chip, unit_chip):
+        own = where[rcv_chip][0] == where[unit_chip][0]
+        return step(rcv_chip, unit_chip) + (0 if own else len(planes[where[rcv_chip][0]]))
+
+    def unit(ch, s):
+        for u in members[ch]:
+            if u == s or topo.may_write(u, s):
+                return u
+        raise ValueError("no unit")
+
+    def relay(s, u):
+        if s == u or topo.may_write(s, u):
+            return None
+        for m in members[topo.chip(s)]:
+            if m != s and topo.may_write(m, u) and topo.may_write(s, m):
+                return m
+        raise ValueError("no relay")
+
+    def hops(s, u):
+        return 0 if s == u else (1 if relay(s, u) is None else 2)
+
+    def served(u):
+        ch = topo.chip(u)
+        ss = [s for s in cores if unit(ch, s) == u]
+        return sorted(ss, key=lambda s: (hops(s, u), topo.chip(s) != ch, step(topo.chip(s), ch), s))
+
+    return dict(chips=chips, members=members, step=step, blk=blk, unit=unit, relay=relay, served=served)
+
+
+def gate_moves(route_r, col_of):
+    left = {}
+    for t, es in enumerate(route_r):
+        for i, e in enumerate(es):
+            left[i * TOK + t] = col_of(e) + t
+    out = []
+    while left:
+        best = None
+        keys = sorted(left)
+        for a in keys:
+            for b in keys:
+                if b <= a or left[b] <= left[a]:
+                    continue
+                ds, dd, n = b - a, left[b] - left[a], 2
+                while left.get(a + n * ds) == left[a] + n * dd:
+                    n += 1
+                if best is None or n > best[4]:
+                    best = (a, ds, left[a], dd, n)
+        if best is None:
+            a = keys[0]
+            best = (a, 1, left[a], 1, 1)
+        out.append(best)
+        for k in range(best[4]):
+            del left[best[0] + k * best[1]]
+    return out
+
+
+def rank_program(g, core, T, topo):
+    rank = T.rank_of(core)
+    if rank is None:
+        return
+    cores = list(T.cores)
+    P = make_plan(cores, topo)
+    sem = T.sem
+    my_chip = topo.chip(core)
+    mates_here = [m for m in P["members"][my_chip] if m != core]
+
+    def masks(c):
+        other = [m for m in P["members"][topo.chip(c)] if m != c][0]
+        away = [d for d in cores if topo.chip(d) != topo.chip(c)][0]
+        full, lo = topo.mask(c, other), topo.mask(c, away)
+        return lo, full & ~lo, full
+
+    def is_relay(c):
+        return any(P["relay"](s, P["unit"](ch, s)) == c for s in cores for ch in P["chips"])
+
+    def w_mask(c):
+        lo, hi, full = masks(c)
+        return hi if is_relay(c) else full
+
+    lo, hi, full = masks(core)
+    sent = [0]
+
+    def send(dst_core, out_ap, in_ap, rsem, mask):
+        rid, pid, _ = topo.addr(dst_core)
+        g.remote_dma(out_ap, in_ap, rsem, sem.sent, pid, rid, mask)
+        sent[0] += _nbits(mask)
+
+    def send_many(dst_cores, out_ap, in_ap, rsem, mask):
+        if len(dst_cores) == 1:
+            send(dst_cores[0], out_ap, in_ap, rsem, mask)
+            return
+        ids = [DstId(rid=topo.addr(d)[0], pnc=topo.addr(d)[1]) for d in dst_cores]
+        g.remote_dma_fused([RemoteDMATransfer(dst_ids=ids, dma_engine_mask=mask, remote_sem=rsem, srcs=[in_ap],
+                                              dsts=[out_ap for _ in dst_cores], alu_op=0)], local_sem=sem.sent)
+        sent[0] += _nbits(mask)
+
+    def slot(r):
+        return T.xu[:, r * TOK:(r + 1) * TOK]
+
+    g.sync.dma_start(T.xo[:], T.x[:]).then_inc(sem.ldx, 16)
+    g.scalar.dma_start(T.g1[0:1, 0:96], T.gate[:]).then_inc(sem.ldg, 16)
+    g.sync.dma_start(T.wo[:, 0:256], T.w1[:]).then_inc(sem.ldw, 16)
+    g.scalar.dma_start(T.wo[:, 256:512], T.w2[:]).then_inc(sem.ldw, 16)
+
+    g.vector.memset(T.ones[0:1, :], 1.0).then_inc(sem.fill, 1)
+    g.vector.memset(T.gd[:, 0:256], 0.0).then_inc(sem.fill, 1)
+    g.vector.memset(T.zero[:], 0.0).then_inc(sem.fill, 1)
+
+    def col_of(e):
+        ec = cores[e]
+        ch = topo.chip(ec)
+        return P["blk"](my_chip, ch) * BLK + P["members"][ch].index(ec) * TOK
+
+    moves = gate_moves(T.tables["ROUTE"][rank], col_of)
+    g.tensor.wait_ge(sem.fill, 3)
+    g.tensor.wait_ge(sem.ldg, 16)
+    for (s0, ds, d0, dd, n) in moves:
+        g.tensor.matmul(T.gd[:, d0:d0 + (n - 1) * dd + 1:dd], T.ones[0:1, :], T.g1[0:1, s0:s0 + (n - 1) * ds + 1:ds],
+                        start=True, stop=True).then_inc(sem.gsc, 1)
+
+    my_units = [P["unit"](ch, core) for ch in P["chips"]]
+    via = sorted(set(P["relay"](core, u) for u in my_units if P["relay"](core, u) is not None))
+    direct = [u for u in my_units if u != core and P["relay"](core, u) is None]
+    d_off = sorted([u for u in direct if topo.chip(u) != my_chip],
+                   key=lambda u: (topo.same_plane(my_chip, topo.chip(u)), P["step"](my_chip, topo.chip(u))))
+    d_on = [u for u in direct if topo.chip(u) == my_chip]
+    g.wait_ge(sem.ldx, 16)
+    for m in via:
+        send(m, T.xr[:], T.xo[:], sem.xrs, lo)
+    if d_off:
+        send_many(d_off, slot(rank), T.xo[:], sem["xs%d" % rank], lo)
+    for u in d_on:
+        send(u, slot(rank), T.xo[:], sem["xs%d" % rank], hi)
+    g.wait_ge(sem.ldw, 32)
+    for m in mates_here:
+        send(m, T.wp[:], T.wo[:], sem.wps, w_mask(core))
+    for s in mates_here:
+        tg = [P["unit"](ch, s) for ch in P["chips"] if P["relay"](s, P["unit"](ch, s)) == core]
+        if tg:
+            tg.sort(key=lambda u: P["step"](my_chip, topo.chip(u)))
+            g.wait_ge(sem.xrs, _nbits(masks(s)[0]))
+            send_many(tg, slot(T.rank_of(s)), T.xr[:], sem["xs%d" % T.rank_of(s)], lo)
+
+    served = P["served"](core)
+    experts = P["members"][my_chip]
+    wbuf = [T.wo if m == core else T.wp for m in experts]
+    own_round = None
+    g.tensor.wait_ge(sem.ldw, 32)
+    for m in mates_here:
+        g.tensor.wait_ge(sem.wps, _nbits(w_mask(m)))
+    g.vector.wait_ge(sem.fill, 3)
+    for n, s in enumerate(served):
+        pb = T["pb%d" % n]
+        sr = T.rank_of(s)
+        if s == core:
+            g.tensor.wait_ge(sem.ldx, 16)
+            xin = T.xo[:]
+        else:
+            writer = P["relay"](s, core) or s
+            g.tensor.wait_ge(sem["xs%d" % sr], _nbits(masks(writer)[1] if topo.chip(s) == my_chip else masks(writer)[0]))
+            xin = slot(sr)
+        for k in range(2):
+            for f in range(2):
+                c = (2 * k + f) * TOK
+                g.tensor.matmul(pb[:, c:c + TOK], wbuf[k][:, 128 * f:128 * f + 128], xin,
+                                start=True, stop=True).then_inc(sem["hh%d" % n], 1)
+        g.vector.wait_ge(sem["hh%d" % n], 4)
+        g.vector.tensor_tensor(T.hs[:, n * 128:(n + 1) * 128], pb[:, 0:128], T.zero[:],
+                               AluOpType.max).then_inc(sem["rl%d" % n], 1)
+        g.tensor.wait_ge(sem["rl%d" % n], 1)
+        for k in range(2):
+            for f in range(2):
+                c = n * 128 + (2 * k + f) * TOK
+                g.tensor.matmul(pb[:, 128 + k * TOK:128 + (k + 1) * TOK], wbuf[k][:, 256 + 128 * f:256 + 128 * f + 128],
+                                T.hs[:, c:c + TOK], start=(f == 0), stop=(f == 1)).then_inc(sem["rr%d" % n], 1)
+        g.vector.wait_ge(sem["rr%d" % n], 4)
+        b = P["blk"](topo.chip(s), my_chip)
+        if s == core:
+            own_round = n
+            g.vector.tensor_copy(T.land[:, b * BLK:(b + 1) * BLK], pb[:, 128:128 + BLK]).then_inc(sem["cp%d" % n], 1)
+        else:
+            g.vector.tensor_copy(T.ro[:, n * BLK:(n + 1) * BLK], pb[:, 128:128 + BLK]).then_inc(sem["cp%d" % n], 1)
+            g.wait_ge(sem["cp%d" % n], 1)
+            send(s, T.land[:, b * BLK:(b + 1) * BLK], T.ro[:, n * BLK:(n + 1) * BLK], sem["ret%d" % b],
+                 hi if topo.chip(s) == my_chip else lo)
+
+    def wait_block(b):
+        ch = [c for c in P["chips"] if P["blk"](my_chip, c) == b][0]
+        u = P["unit"](ch, core)
+        if u == core:
+            g.vector.wait_ge(sem["cp%d" % own_round], 1)
+        else:
+            g.vector.wait_ge(sem["ret%d" % b], _nbits(masks(u)[1] if ch == my_chip else masks(u)[0]))
+
+    done = [0]
+
+    def vop(out, in0, in1, op):
+        g.vector.tensor_tensor(out, in0, in1, op).then_inc(sem.cmb, 1)
+        done[0] += 1
+
+    def vsync():
+        g.vector.wait_ge(sem.cmb, done[0])
+
+    g.vector.wait_ge(sem.gsc, len(moves))
+    wait_block(0)
+    wait_block(1)
+    vop(T.pr[:, 0:2 * BLK], T.land[:, 0:2 * BLK], T.gd[:, 0:2 * BLK], AluOpType.mult)
+    vsync()
+    vop(T.gd[:, 256:256 + BLK], T.pr[:, 0:BLK], T.pr[:, BLK:2 * BLK], AluOpType.add)
+    wait_block(2)
+    vop(T.pr[:, 2 * BLK:3 * BLK], T.land[:, 2 * BLK:3 * BLK], T.gd[:, 2 * BLK:3 * BLK], AluOpType.mult)
+    vsync()
+    vop(T.gd[:, 320:320 + BLK], T.pr[:, 2 * BLK:3 * BLK], T.gd[:, 256:256 + BLK], AluOpType.add)
+    wait_block(3)
+    vop(T.pr[:, 3 * BLK:4 * BLK], T.land[:, 3 * BLK:4 * BLK], T.gd[:, 3 * BLK:4 * BLK], AluOpType.mult)
+    vsync()
+    vop(T.s3[:], T.pr[:, 3 * BLK:4 * BLK], T.gd[:, 320:320 + BLK], AluOpType.add)
+    vsync()
+    g.vector.tensor_tensor(T.yo[:], T.s3[:, 0:TOK], T.s3[:, TOK:BLK], AluOpType.add).then_inc(sem.yv, 1)
+    g.sync.wait_ge(sem.yv, 1)
+    g.sync.dma_start(T.y[:], T.yo[:]).then_inc(sem.stored, 16)
+    g.sync.wait_ge(sem.stored, 16)
+    g.wait_ge(sem.sent, sent[0])

@@ -2,34 +2,40 @@ from concourse.bass import DstId, RemoteDMATransfer
 from concourse.mybir import AluOpType
 
 NRANK = 8
-NROUND = 4
+NSRC = 4
+NJOB = 4
 TOK = 32
 BLK = 2 * TOK
+NHEAD = 4
 
 SCRATCH = {
     "xo": ("sbuf", [128, TOK], "bfloat16"),
-    "xr": ("sbuf", [128, TOK], "bfloat16"),
-    "xu": ("sbuf", [128, NRANK * TOK], "bfloat16"),
+    "xd": ("dram", [128, TOK], "bfloat16"),
+    "xr": ("dram", [128, TOK], "bfloat16"),
+    "xu": ("sbuf", [128, NSRC * TOK], "bfloat16"),
     "wo": ("sbuf", [128, 512], "bfloat16"),
     "wp": ("sbuf", [128, 512], "bfloat16"),
     "zero": ("sbuf", [128, 128], "float32"),
     "ones": ("sbuf", [128, 128], "bfloat16"),
     "g1": ("sbuf", [128, 96], "bfloat16"),
-    "hs": ("sbuf", [128, NROUND * 128], "bfloat16"),
-    "ro": ("sbuf", [128, NROUND * BLK], "bfloat16"),
+    "gs": ("sbuf", [128, 256], "bfloat16"),
+    "hs": ("sbuf", [128, NJOB * 128], "bfloat16"),
+    "ro": ("sbuf", [128, NSRC * BLK], "bfloat16"),
     "land": ("sbuf", [128, 4 * BLK], "bfloat16"),
     "pr": ("sbuf", [128, 4 * BLK], "float32"),
     "s3": ("sbuf", [128, BLK], "float32"),
     "yo": ("sbuf", [128, TOK], "bfloat16"),
+    "gr": ("psum", [128, 512], "float32"),
     "gd": ("psum", [128, 512], "float32"),
     "pb0": ("psum", [128, 512], "float32"),
     "pb1": ("psum", [128, 512], "float32"),
     "pb2": ("psum", [128, 512], "float32"),
     "pb3": ("psum", [128, 512], "float32"),
 }
-SEMAPHORES = (["ldx", "ldw", "ldg", "fill", "gsc", "xrs", "wps", "sent", "cmb", "yv", "stored"]
+SEMAPHORES = (["ldx", "ldd", "ldw1", "ldw2", "ldg", "fill", "gsc", "gcp", "gbc", "xrs", "wps", "sent", "cmb", "yv",
+               "stored"]
               + ["xs%d" % r for r in range(NRANK)] + ["ret%d" % j for j in range(4)]
-              + ["%s%d" % (s, n) for s in ("hh", "rl", "rr", "cp") for n in range(NROUND)])
+              + ["%s%d" % (s, n) for s in ("hh", "rl", "rr", "cp") for n in range(4)])
 
 
 def _bits(mask):
@@ -129,6 +135,9 @@ def rank_program(g, core, T, topo):
         full, lo = topo.mask(c, other), topo.mask(c, away)
         return lo, full & ~lo, full
 
+    def head_mask(c):
+        return sum(1 << k for k in _bits(masks(c)[0])[:NHEAD])
+
     def is_relay(c):
         return any(P["relay"](s, P["unit"](ch, s)) == c for s in cores for ch in P["chips"])
 
@@ -144,25 +153,36 @@ def rank_program(g, core, T, topo):
         g.remote_dma(out_ap, in_ap, rsem, sem.sent, pid, rid, mask)
         sent[0] += _nbits(mask)
 
-    def send_many(dst_cores, out_ap, in_ap, rsem, mask):
-        if len(dst_cores) == 1:
-            send(dst_cores[0], out_ap, in_ap, rsem, mask)
+    def slot(u, s):
+        n = P["served"](u).index(s)
+        return T.xu[:, n * TOK:(n + 1) * TOK]
+
+    def send_x(units, s, in_ap, mask):
+        rsem = sem["xs%d" % T.rank_of(s)]
+        if len(units) == 1:
+            send(units[0], slot(units[0], s), in_ap, rsem, mask)
             return
-        ids = [DstId(rid=topo.addr(d)[0], pnc=topo.addr(d)[1]) for d in dst_cores]
+        ids = [DstId(rid=topo.addr(d)[0], pnc=topo.addr(d)[1]) for d in units]
         g.remote_dma_fused([RemoteDMATransfer(dst_ids=ids, dma_engine_mask=mask, remote_sem=rsem, srcs=[in_ap],
-                                              dsts=[out_ap for _ in dst_cores], alu_op=0)], local_sem=sem.sent)
+                                              dsts=[slot(d, s) for d in units], alu_op=0)], local_sem=sem.sent)
         sent[0] += _nbits(mask)
 
-    def slot(r):
-        return T.xu[:, r * TOK:(r + 1) * TOK]
+    served = P["served"](core)
+    xown = slot(core, core) if core in served else T.xo[:]
+    my_units = [P["unit"](ch, core) for ch in P["chips"]]
+    via = sorted(set(P["relay"](core, u) for u in my_units if P["relay"](core, u) is not None))
 
-    g.sync.dma_start(T.xo[:], T.x[:]).then_inc(sem.ldx, 16)
+    if via:
+        g.sync.dma_start(T.xd[:], T.x[:]).then_inc(sem.ldd, 16)
+        g.scalar.dma_start(xown, T.x[:]).then_inc(sem.ldx, 16)
+    else:
+        g.sync.dma_start(xown, T.x[:]).then_inc(sem.ldx, 16)
     g.scalar.dma_start(T.g1[0:1, 0:96], T.gate[:]).then_inc(sem.ldg, 16)
-    g.sync.dma_start(T.wo[:, 0:256], T.w1[:]).then_inc(sem.ldw, 16)
-    g.scalar.dma_start(T.wo[:, 256:512], T.w2[:]).then_inc(sem.ldw, 16)
+    g.sync.dma_start(T.wo[:, 0:256], T.w1[:]).then_inc(sem.ldw1, 16)
+    g.scalar.dma_start(T.wo[:, 256:512], T.w2[:]).then_inc(sem.ldw2, 16)
 
     g.vector.memset(T.ones[0:1, :], 1.0).then_inc(sem.fill, 1)
-    g.vector.memset(T.gd[:, 0:256], 0.0).then_inc(sem.fill, 1)
+    g.vector.memset(T.gr[0:1, 0:256], 0.0).then_inc(sem.fill, 1)
     g.vector.memset(T.zero[:], 0.0).then_inc(sem.fill, 1)
 
     def col_of(e):
@@ -174,80 +194,154 @@ def rank_program(g, core, T, topo):
     g.tensor.wait_ge(sem.fill, 3)
     g.tensor.wait_ge(sem.ldg, 16)
     for (s0, ds, d0, dd, n) in moves:
-        g.tensor.matmul(T.gd[:, d0:d0 + (n - 1) * dd + 1:dd], T.ones[0:1, :], T.g1[0:1, s0:s0 + (n - 1) * ds + 1:ds],
+        g.tensor.matmul(T.gr[0:1, d0:d0 + (n - 1) * dd + 1:dd], T.ones[0:1, 0:1], T.g1[0:1, s0:s0 + (n - 1) * ds + 1:ds],
                         start=True, stop=True).then_inc(sem.gsc, 1)
+    g.vector.wait_ge(sem.fill, 3)
+    g.vector.wait_ge(sem.gsc, len(moves))
+    g.vector.tensor_copy(T.gs[0:1, 0:256], T.gr[0:1, 0:256]).then_inc(sem.gcp, 1)
+    g.tensor.wait_ge(sem.gcp, 1)
+    g.tensor.matmul(T.gd[:, 0:256], T.ones[0:1, :], T.gs[0:1, 0:256], start=True, stop=True).then_inc(sem.gbc, 1)
 
-    my_units = [P["unit"](ch, core) for ch in P["chips"]]
-    via = sorted(set(P["relay"](core, u) for u in my_units if P["relay"](core, u) is not None))
     direct = [u for u in my_units if u != core and P["relay"](core, u) is None]
     d_off = sorted([u for u in direct if topo.chip(u) != my_chip],
                    key=lambda u: (topo.same_plane(my_chip, topo.chip(u)), P["step"](my_chip, topo.chip(u))))
     d_on = [u for u in direct if topo.chip(u) == my_chip]
+    if via:
+        g.wait_ge(sem.ldd, 16)
+        for m in via:
+            send(m, T.xr[:], T.xd[:], sem.xrs, head_mask(core))
     g.wait_ge(sem.ldx, 16)
-    for m in via:
-        send(m, T.xr[:], T.xo[:], sem.xrs, lo)
     if d_off:
-        send_many(d_off, slot(rank), T.xo[:], sem["xs%d" % rank], lo)
+        send_x(d_off, core, xown, lo)
     for u in d_on:
-        send(u, slot(rank), T.xo[:], sem["xs%d" % rank], hi)
-    g.wait_ge(sem.ldw, 32)
+        send_x([u], core, xown, hi)
+    g.wait_ge(sem.ldw1, 16)
+    g.wait_ge(sem.ldw2, 16)
     for m in mates_here:
         send(m, T.wp[:], T.wo[:], sem.wps, w_mask(core))
     for s in mates_here:
         tg = [P["unit"](ch, s) for ch in P["chips"] if P["relay"](s, P["unit"](ch, s)) == core]
         if tg:
             tg.sort(key=lambda u: P["step"](my_chip, topo.chip(u)))
-            g.wait_ge(sem.xrs, _nbits(masks(s)[0]))
-            send_many(tg, slot(T.rank_of(s)), T.xr[:], sem["xs%d" % T.rank_of(s)], lo)
+            g.wait_ge(sem.xrs, _nbits(head_mask(s)))
+            send_x(tg, s, T.xr[:], lo)
 
-    served = P["served"](core)
     experts = P["members"][my_chip]
     wbuf = [T.wo if m == core else T.wp for m in experts]
-    own_round = None
-    g.tensor.wait_ge(sem.ldw, 32)
-    for m in mates_here:
-        g.tensor.wait_ge(sem.wps, _nbits(w_mask(m)))
-    g.vector.wait_ge(sem.fill, 3)
-    for n, s in enumerate(served):
-        pb = T["pb%d" % n]
-        sr = T.rank_of(s)
+    ko = experts.index(core)
+    kp = 1 - ko
+    pairs = [served[0:2], served[2:4]]
+    late = any(P["relay"](s, core) is not None for s in served)
+    have = {}
+
+    def need_x(s):
+        if ("x", s) in have:
+            return
+        have[("x", s)] = 1
         if s == core:
             g.tensor.wait_ge(sem.ldx, 16)
-            xin = T.xo[:]
         else:
             writer = P["relay"](s, core) or s
-            g.tensor.wait_ge(sem["xs%d" % sr], _nbits(masks(writer)[1] if topo.chip(s) == my_chip else masks(writer)[0]))
-            xin = slot(sr)
+            g.tensor.wait_ge(sem["xs%d" % T.rank_of(s)],
+                             _nbits(masks(writer)[1] if topo.chip(s) == my_chip else masks(writer)[0]))
+
+    def need_w(k, stage):
+        key = ("w", k, stage if k == ko else 0)
+        if key in have:
+            return
+        have[key] = 1
+        if k == ko:
+            g.tensor.wait_ge(sem["ldw%d" % stage], 16)
+        else:
+            for m in mates_here:
+                g.tensor.wait_ge(sem.wps, _nbits(w_mask(m)))
+
+    def relu(j, nmm):
+        pb = T["pb%d" % j]
+        g.vector.wait_ge(sem["hh%d" % j], nmm)
+        g.vector.tensor_tensor(T.hs[:, j * 128:(j + 1) * 128], pb[:, 0:128], T.zero[:],
+                               AluOpType.max).then_inc(sem["rl%d" % j], 1)
+
+    def stage1(j, p, k):
+        pb = T["pb%d" % j]
+        for s in pairs[p]:
+            need_x(s)
+        need_w(k, 1)
+        for f in range(2):
+            g.tensor.matmul(pb[:, f * BLK:(f + 1) * BLK], wbuf[k][:, 128 * f:128 * f + 128], T.xu[:, p * BLK:(p + 1) * BLK],
+                            start=True, stop=True).then_inc(sem["hh%d" % j], 1)
+        relu(j, 2)
+
+    def stage2(j, p, k):
+        pb = T["pb%d" % j]
+        need_w(k, 2)
+        g.tensor.wait_ge(sem["rl%d" % j], 1)
+        for f in range(2):
+            c = j * 128 + f * BLK
+            g.tensor.matmul(pb[:, 128:128 + BLK], wbuf[k][:, 256 + 128 * f:256 + 128 * f + 128], T.hs[:, c:c + BLK],
+                            start=(f == 0), stop=(f == 1)).then_inc(sem["rr%d" % j], 1)
+        g.vector.wait_ge(sem["rr%d" % j], 2)
+        for i, s in enumerate(pairs[p]):
+            n = 2 * p + i
+            if s == core:
+                c = P["blk"](my_chip, my_chip) * BLK + k * TOK
+                out = T.land[:, c:c + TOK]
+            else:
+                c = n * BLK + k * TOK
+                out = T.ro[:, c:c + TOK]
+            g.vector.tensor_copy(out, pb[:, 128 + i * TOK:128 + (i + 1) * TOK]).then_inc(sem["cp%d" % n], 1)
+
+    def single(j, n):
+        pb = T["pb%d" % j]
+        need_x(served[n])
+        for k in range(2):
+            need_w(k, 1)
+            need_w(k, 2)
         for k in range(2):
             for f in range(2):
                 c = (2 * k + f) * TOK
-                g.tensor.matmul(pb[:, c:c + TOK], wbuf[k][:, 128 * f:128 * f + 128], xin,
-                                start=True, stop=True).then_inc(sem["hh%d" % n], 1)
-        g.vector.wait_ge(sem["hh%d" % n], 4)
-        g.vector.tensor_tensor(T.hs[:, n * 128:(n + 1) * 128], pb[:, 0:128], T.zero[:],
-                               AluOpType.max).then_inc(sem["rl%d" % n], 1)
-        g.tensor.wait_ge(sem["rl%d" % n], 1)
+                g.tensor.matmul(pb[:, c:c + TOK], wbuf[k][:, 128 * f:128 * f + 128], T.xu[:, n * TOK:(n + 1) * TOK],
+                                start=True, stop=True).then_inc(sem["hh%d" % j], 1)
+        relu(j, 4)
+        g.tensor.wait_ge(sem["rl%d" % j], 1)
         for k in range(2):
             for f in range(2):
-                c = n * 128 + (2 * k + f) * TOK
+                c = j * 128 + (2 * k + f) * TOK
                 g.tensor.matmul(pb[:, 128 + k * TOK:128 + (k + 1) * TOK], wbuf[k][:, 256 + 128 * f:256 + 128 * f + 128],
-                                T.hs[:, c:c + TOK], start=(f == 0), stop=(f == 1)).then_inc(sem["rr%d" % n], 1)
-        g.vector.wait_ge(sem["rr%d" % n], 4)
-        b = P["blk"](topo.chip(s), my_chip)
+                                T.hs[:, c:c + TOK], start=(f == 0), stop=(f == 1)).then_inc(sem["rr%d" % j], 1)
+        g.vector.wait_ge(sem["rr%d" % j], 4)
+        g.vector.tensor_copy(T.ro[:, n * BLK:(n + 1) * BLK], pb[:, 128:128 + BLK]).then_inc(sem["cp%d" % n], 2)
+
+    def two(ja, jb):
+        stage1(*ja)
+        stage1(*jb)
+        stage2(*ja)
+        stage2(*jb)
+
+    if late:
+        two((0, 0, ko), (1, 0, kp))
+        single(2, 2)
+        single(3, 3)
+        back = [0, 1, 2, 3]
+    else:
+        two((0, 0, ko), (1, 1, ko))
+        two((2, 1, kp), (3, 0, kp))
+        back = [2, 3, 0, 1]
+
+    for n in back:
+        s = served[n]
         if s == core:
-            own_round = n
-            g.vector.tensor_copy(T.land[:, b * BLK:(b + 1) * BLK], pb[:, 128:128 + BLK]).then_inc(sem["cp%d" % n], 1)
-        else:
-            g.vector.tensor_copy(T.ro[:, n * BLK:(n + 1) * BLK], pb[:, 128:128 + BLK]).then_inc(sem["cp%d" % n], 1)
-            g.wait_ge(sem["cp%d" % n], 1)
-            send(s, T.land[:, b * BLK:(b + 1) * BLK], T.ro[:, n * BLK:(n + 1) * BLK], sem["ret%d" % b],
-                 hi if topo.chip(s) == my_chip else lo)
+            continue
+        b = P["blk"](topo.chip(s), my_chip)
+        g.wait_ge(sem["cp%d" % n], 2)
+        send(s, T.land[:, b * BLK:(b + 1) * BLK], T.ro[:, n * BLK:(n + 1) * BLK], sem["ret%d" % b],
+             hi if topo.chip(s) == my_chip else lo)
 
     def wait_block(b):
         ch = [c for c in P["chips"] if P["blk"](my_chip, c) == b][0]
         u = P["unit"](ch, core)
         if u == core:
-            g.vector.wait_ge(sem["cp%d" % own_round], 1)
+            g.vector.wait_ge(sem["cp%d" % served.index(core)], 2)
         else:
             g.vector.wait_ge(sem["ret%d" % b], _nbits(masks(u)[1] if ch == my_chip else masks(u)[0]))
 
@@ -260,20 +354,21 @@ def rank_program(g, core, T, topo):
     def vsync():
         g.vector.wait_ge(sem.cmb, done[0])
 
-    g.vector.wait_ge(sem.gsc, len(moves))
-    wait_block(0)
-    wait_block(1)
-    vop(T.pr[:, 0:2 * BLK], T.land[:, 0:2 * BLK], T.gd[:, 0:2 * BLK], AluOpType.mult)
-    vsync()
-    vop(T.gd[:, 256:256 + BLK], T.pr[:, 0:BLK], T.pr[:, BLK:2 * BLK], AluOpType.add)
-    wait_block(2)
-    vop(T.pr[:, 2 * BLK:3 * BLK], T.land[:, 2 * BLK:3 * BLK], T.gd[:, 2 * BLK:3 * BLK], AluOpType.mult)
-    vsync()
-    vop(T.gd[:, 320:320 + BLK], T.pr[:, 2 * BLK:3 * BLK], T.gd[:, 256:256 + BLK], AluOpType.add)
-    wait_block(3)
-    vop(T.pr[:, 3 * BLK:4 * BLK], T.land[:, 3 * BLK:4 * BLK], T.gd[:, 3 * BLK:4 * BLK], AluOpType.mult)
-    vsync()
-    vop(T.s3[:], T.pr[:, 3 * BLK:4 * BLK], T.gd[:, 320:320 + BLK], AluOpType.add)
+    order = [0, 1, 2, 3] if via else [2, 3, 1, 0]
+    part = [T.gd[:, 256:256 + BLK], T.gd[:, 320:320 + BLK]]
+    g.vector.wait_ge(sem.gbc, 1)
+    prev = None
+    for i, b in enumerate(order):
+        prb = T.pr[:, b * BLK:(b + 1) * BLK]
+        wait_block(b)
+        vop(prb, T.land[:, b * BLK:(b + 1) * BLK], T.gd[:, b * BLK:(b + 1) * BLK], AluOpType.mult)
+        vsync()
+        if i == 0:
+            prev = prb
+        else:
+            out = T.s3[:] if i == len(order) - 1 else part[i % 2]
+            vop(out, prb, prev, AluOpType.add)
+            prev = out
     vsync()
     g.vector.tensor_tensor(T.yo[:], T.s3[:, 0:TOK], T.s3[:, TOK:BLK], AluOpType.add).then_inc(sem.yv, 1)
     g.sync.wait_ge(sem.yv, 1)

from concourse.bass import DstId, RemoteDMATransfer
from concourse.mybir import AluOpType

NRANK = 8
NSRC = 4
NJOB = 4
TOK = 32
BLK = 2 * TOK
NHEAD = 4

SCRATCH = {
    "xo": ("sbuf", [128, TOK], "bfloat16"),
    "xd": ("dram", [128, TOK], "bfloat16"),
    "xr": ("dram", [128, TOK], "bfloat16"),
    "xu": ("sbuf", [128, NSRC * TOK], "bfloat16"),
    "wo": ("sbuf", [128, 512], "bfloat16"),
    "wp": ("sbuf", [128, 512], "bfloat16"),
    "zero": ("sbuf", [128, 128], "float32"),
    "ones": ("sbuf", [128, 128], "bfloat16"),
    "g1": ("sbuf", [128, 96], "bfloat16"),
    "gs": ("sbuf", [128, 256], "bfloat16"),
    "hs": ("sbuf", [128, NJOB * 128], "bfloat16"),
    "ro": ("sbuf", [128, NSRC * BLK], "bfloat16"),
    "land": ("sbuf", [128, 4 * BLK], "bfloat16"),
    "pr": ("sbuf", [128, 4 * BLK], "float32"),
    "s3": ("sbuf", [128, BLK], "float32"),
    "yo": ("sbuf", [128, TOK], "bfloat16"),
    "gr": ("psum", [128, 512], "float32"),
    "gd": ("psum", [128, 512], "float32"),
    "pb0": ("psum", [128, 512], "float32"),
    "pb1": ("psum", [128, 512], "float32"),
    "pb2": ("psum", [128, 512], "float32"),
    "pb3": ("psum", [128, 512], "float32"),
}
SEMAPHORES = (["ldx", "ldd", "ldw1", "ldw2", "ldg", "fill", "gsc", "gcp", "gbc", "xrs", "wps", "sent", "cmb", "yv",
               "stored"]
              + ["xs%d" % r for r in range(NRANK)] + ["ret%d" % j for j in range(4)]
              + ["%s%d" % (s, n) for s in ("hh", "rl", "rr", "cp") for n in range(4)])


def _bits(mask):
    return [k for k in range(16) if (mask >> k) & 1]


def _nbits(mask):
    return len(_bits(mask))


def make_plan(cores, topo):
    chips = sorted(set(topo.chip(c) for c in cores))
    reach = lambda c: sum(1 for d in cores if d != c and topo.may_write(c, d))
    members = {ch: sorted([c for c in cores if topo.chip(c) == ch], key=lambda c: (reach(c), c)) for ch in chips}
    planes = []
    for ch in chips:
        for grp in planes:
            if topo.same_plane(grp[0], ch):
                grp.append(ch)
                break
        else:
            planes.append([ch])
    where = {ch: (gi, grp.index(ch)) for gi, grp in enumerate(planes) for ch in grp}

    def step(src_chip, dst_chip):
        return (where[dst_chip][1] - where[src_chip][1]) % len(planes[where[dst_chip][0]])

    def blk(rcv_chip, unit_chip):
        own = where[rcv_chip][0] == where[unit_chip][0]
        return step(rcv_chip, unit_chip) + (0 if own else len(planes[where[rcv_chip][0]]))

    def unit(ch, s):
        for u in members[ch]:
            if u == s or topo.may_write(u, s):
                return u
        raise ValueError("no unit")

    def relay(s, u):
        if s == u or topo.may_write(s, u):
            return None
        for m in members[topo.chip(s)]:
            if m != s and topo.may_write(m, u) and topo.may_write(s, m):
                return m
        raise ValueError("no relay")

    def hops(s, u):
        return 0 if s == u else (1 if relay(s, u) is None else 2)

    def served(u):
        ch = topo.chip(u)
        ss = [s for s in cores if unit(ch, s) == u]
        return sorted(ss, key=lambda s: (hops(s, u), topo.chip(s) != ch, step(topo.chip(s), ch), s))

    return dict(chips=chips, members=members, step=step, blk=blk, unit=unit, relay=relay, served=served)


def gate_moves(route_r, col_of):
    left = {}
    for t, es in enumerate(route_r):
        for i, e in enumerate(es):
            left[i * TOK + t] = col_of(e) + t
    out = []
    while left:
        best = None
        keys = sorted(left)
        for a in keys:
            for b in keys:
                if b <= a or left[b] <= left[a]:
                    continue
                ds, dd, n = b - a, left[b] - left[a], 2
                while left.get(a + n * ds) == left[a] + n * dd:
                    n += 1
                if best is None or n > best[4]:
                    best = (a, ds, left[a], dd, n)
        if best is None:
            a = keys[0]
            best = (a, 1, left[a], 1, 1)
        out.append(best)
        for k in range(best[4]):
            del left[best[0] + k * best[1]]
    return out


def rank_program(g, core, T, topo):
    rank = T.rank_of(core)
    if rank is None:
        return
    cores = list(T.cores)
    P = make_plan(cores, topo)
    sem = T.sem
    my_chip = topo.chip(core)
    mates_here = [m for m in P["members"][my_chip] if m != core]

    def masks(c):
        other = [m for m in P["members"][topo.chip(c)] if m != c][0]
        away = [d for d in cores if topo.chip(d) != topo.chip(c)][0]
        full, lo = topo.mask(c, other), topo.mask(c, away)
        return lo, full & ~lo, full

    def head_mask(c):
        return sum(1 << k for k in _bits(masks(c)[0])[:NHEAD])

    def is_relay(c):
        return any(P["relay"](s, P["unit"](ch, s)) == c for s in cores for ch in P["chips"])

    def w_mask(c):
        lo, hi, full = masks(c)
        return hi if is_relay(c) else full

    lo, hi, full = masks(core)
    sent = [0]

    def send(dst_core, out_ap, in_ap, rsem, mask):
        rid, pid, _ = topo.addr(dst_core)
        g.remote_dma(out_ap, in_ap, rsem, sem.sent, pid, rid, mask)
        sent[0] += _nbits(mask)

    def slot(u, s):
        n = P["served"](u).index(s)
        return T.xu[:, n * TOK:(n + 1) * TOK]

    def send_x(units, s, in_ap, mask):
        rsem = sem["xs%d" % T.rank_of(s)]
        if len(units) == 1:
            send(units[0], slot(units[0], s), in_ap, rsem, mask)
            return
        ids = [DstId(rid=topo.addr(d)[0], pnc=topo.addr(d)[1]) for d in units]
        g.remote_dma_fused([RemoteDMATransfer(dst_ids=ids, dma_engine_mask=mask, remote_sem=rsem, srcs=[in_ap],
                                              dsts=[slot(d, s) for d in units], alu_op=0)], local_sem=sem.sent)
        sent[0] += _nbits(mask)

    served = P["served"](core)
    xown = slot(core, core) if core in served else T.xo[:]
    my_units = [P["unit"](ch, core) for ch in P["chips"]]
    via = sorted(set(P["relay"](core, u) for u in my_units if P["relay"](core, u) is not None))

    if via:
        g.sync.dma_start(T.xd[:], T.x[:]).then_inc(sem.ldd, 16)
        g.scalar.dma_start(xown, T.x[:]).then_inc(sem.ldx, 16)
    else:
        g.sync.dma_start(xown, T.x[:]).then_inc(sem.ldx, 16)
    g.scalar.dma_start(T.g1[0:1, 0:96], T.gate[:]).then_inc(sem.ldg, 16)
    g.sync.dma_start(T.wo[:, 0:256], T.w1[:]).then_inc(sem.ldw1, 16)
    g.scalar.dma_start(T.wo[:, 256:512], T.w2[:]).then_inc(sem.ldw2, 16)

    g.vector.memset(T.ones[0:1, :], 1.0).then_inc(sem.fill, 1)
    g.vector.memset(T.gr[0:1, 0:256], 0.0).then_inc(sem.fill, 1)
    g.vector.memset(T.zero[:], 0.0).then_inc(sem.fill, 1)

    def col_of(e):
        ec = cores[e]
        ch = topo.chip(ec)
        return P["blk"](my_chip, ch) * BLK + P["members"][ch].index(ec) * TOK

    moves = gate_moves(T.tables["ROUTE"][rank], col_of)
    g.tensor.wait_ge(sem.fill, 3)
    g.tensor.wait_ge(sem.ldg, 16)
    for (s0, ds, d0, dd, n) in moves:
        g.tensor.matmul(T.gr[0:1, d0:d0 + (n - 1) * dd + 1:dd], T.ones[0:1, 0:1], T.g1[0:1, s0:s0 + (n - 1) * ds + 1:ds],
                        start=True, stop=True).then_inc(sem.gsc, 1)
    g.vector.wait_ge(sem.fill, 3)
    g.vector.wait_ge(sem.gsc, len(moves))
    g.vector.tensor_copy(T.gs[0:1, 0:256], T.gr[0:1, 0:256]).then_inc(sem.gcp, 1)
    g.tensor.wait_ge(sem.gcp, 1)
    g.tensor.matmul(T.gd[:, 0:256], T.ones[0:1, :], T.gs[0:1, 0:256], start=True, stop=True).then_inc(sem.gbc, 1)

    direct = [u for u in my_units if u != core and P["relay"](core, u) is None]
    d_off = sorted([u for u in direct if topo.chip(u) != my_chip],
                   key=lambda u: (topo.same_plane(my_chip, topo.chip(u)), P["step"](my_chip, topo.chip(u))))
    d_on = [u for u in direct if topo.chip(u) == my_chip]
    if via:
        g.wait_ge(sem.ldd, 16)
        for m in via:
            send(m, T.xr[:], T.xd[:], sem.xrs, head_mask(core))
    g.wait_ge(sem.ldx, 16)
    if d_off:
        send_x(d_off, core, xown, lo)
    for u in d_on:
        send_x([u], core, xown, hi)
    g.wait_ge(sem.ldw1, 16)
    g.wait_ge(sem.ldw2, 16)
    for m in mates_here:
        send(m, T.wp[:], T.wo[:], sem.wps, w_mask(core))
    for s in mates_here:
        tg = [P["unit"](ch, s) for ch in P["chips"] if P["relay"](s, P["unit"](ch, s)) == core]
        if tg:
            tg.sort(key=lambda u: P["step"](my_chip, topo.chip(u)))
            g.wait_ge(sem.xrs, _nbits(head_mask(s)))
            send_x(tg, s, T.xr[:], lo)

    experts = P["members"][my_chip]
    wbuf = [T.wo if m == core else T.wp for m in experts]
    ko = experts.index(core)
    kp = 1 - ko
    pairs = [served[0:2], served[2:4]]
    late = any(P["relay"](s, core) is not None for s in served)
    have = {}

    def need_x(s):
        if ("x", s) in have:
            return
        have[("x", s)] = 1
        if s == core:
            g.tensor.wait_ge(sem.ldx, 16)
        else:
            writer = P["relay"](s, core) or s
            g.tensor.wait_ge(sem["xs%d" % T.rank_of(s)],
                             _nbits(masks(writer)[1] if topo.chip(s) == my_chip else masks(writer)[0]))

    def need_w(k, stage):
        key = ("w", k, stage if k == ko else 0)
        if key in have:
            return
        have[key] = 1
        if k == ko:
            g.tensor.wait_ge(sem["ldw%d" % stage], 16)
        else:
            for m in mates_here:
                g.tensor.wait_ge(sem.wps, _nbits(w_mask(m)))

    def relu(j, nmm):
        pb = T["pb%d" % j]
        g.vector.wait_ge(sem["hh%d" % j], nmm)
        g.vector.tensor_tensor(T.hs[:, j * 128:(j + 1) * 128], pb[:, 0:128], T.zero[:],
                               AluOpType.max).then_inc(sem["rl%d" % j], 1)

    def stage1(j, p, k):
        pb = T["pb%d" % j]
        for s in pairs[p]:
            need_x(s)
        need_w(k, 1)
        for f in range(2):
            g.tensor.matmul(pb[:, f * BLK:(f + 1) * BLK], wbuf[k][:, 128 * f:128 * f + 128], T.xu[:, p * BLK:(p + 1) * BLK],
                            start=True, stop=True).then_inc(sem["hh%d" % j], 1)
        relu(j, 2)

    def stage2(j, p, k):
        pb = T["pb%d" % j]
        need_w(k, 2)
        g.tensor.wait_ge(sem["rl%d" % j], 1)
        for f in range(2):
            c = j * 128 + f * BLK
            g.tensor.matmul(pb[:, 128:128 + BLK], wbuf[k][:, 256 + 128 * f:256 + 128 * f + 128], T.hs[:, c:c + BLK],
                            start=(f == 0), stop=(f == 1)).then_inc(sem["rr%d" % j], 1)
        g.vector.wait_ge(sem["rr%d" % j], 2)
        for i, s in enumerate(pairs[p]):
            n = 2 * p + i
            if s == core:
                c = P["blk"](my_chip, my_chip) * BLK + k * TOK
                out = T.land[:, c:c + TOK]
            else:
                c = n * BLK + k * TOK
                out = T.ro[:, c:c + TOK]
            g.vector.tensor_copy(out, pb[:, 128 + i * TOK:128 + (i + 1) * TOK]).then_inc(sem["cp%d" % n], 1)

    def single(j, n):
        pb = T["pb%d" % j]
        need_x(served[n])
        for k in range(2):
            need_w(k, 1)
            need_w(k, 2)
        for k in range(2):
            for f in range(2):
                c = (2 * k + f) * TOK
                g.tensor.matmul(pb[:, c:c + TOK], wbuf[k][:, 128 * f:128 * f + 128], T.xu[:, n * TOK:(n + 1) * TOK],
                                start=True, stop=True).then_inc(sem["hh%d" % j], 1)
        relu(j, 4)
        g.tensor.wait_ge(sem["rl%d" % j], 1)
        for k in range(2):
            for f in range(2):
                c = j * 128 + (2 * k + f) * TOK
                g.tensor.matmul(pb[:, 128 + k * TOK:128 + (k + 1) * TOK], wbuf[k][:, 256 + 128 * f:256 + 128 * f + 128],
                                T.hs[:, c:c + TOK], start=(f == 0), stop=(f == 1)).then_inc(sem["rr%d" % j], 1)
        g.vector.wait_ge(sem["rr%d" % j], 4)
        g.vector.tensor_copy(T.ro[:, n * BLK:(n + 1) * BLK], pb[:, 128:128 + BLK]).then_inc(sem["cp%d" % n], 2)

    def two(ja, jb):
        stage1(*ja)
        stage1(*jb)
        stage2(*ja)
        stage2(*jb)

    if late:
        two((0, 0, ko), (1, 0, kp))
        single(2, 2)
        single(3, 3)
        back = [0, 1, 2, 3]
    else:
        two((0, 0, ko), (1, 1, ko))
        two((2, 1, kp), (3, 0, kp))
        back = [2, 3, 0, 1]

    for n in back:
        s = served[n]
        if s == core:
            continue
        b = P["blk"](topo.chip(s), my_chip)
        g.wait_ge(sem["cp%d" % n], 2)
        send(s, T.land[:, b * BLK:(b + 1) * BLK], T.ro[:, n * BLK:(n + 1) * BLK], sem["ret%d" % b],
             hi if topo.chip(s) == my_chip else lo)

    def wait_block(b):
        ch = [c for c in P["chips"] if P["blk"](my_chip, c) == b][0]
        u = P["unit"](ch, core)
        if u == core:
            g.vector.wait_ge(sem["cp%d" % served.index(core)], 2)
        else:
            g.vector.wait_ge(sem["ret%d" % b], _nbits(masks(u)[1] if ch == my_chip else masks(u)[0]))

    done = [0]

    def vop(out, in0, in1, op):
        g.vector.tensor_tensor(out, in0, in1, op).then_inc(sem.cmb, 1)
        done[0] += 1

    def vsync():
        g.vector.wait_ge(sem.cmb, done[0])

    order = [0, 1, 2, 3] if via else [2, 3, 1, 0]
    part = [T.gd[:, 256:256 + BLK], T.gd[:, 320:320 + BLK]]
    g.vector.wait_ge(sem.gbc, 1)
    prev = None
    for i, b in enumerate(order):
        prb = T.pr[:, b * BLK:(b + 1) * BLK]
        wait_block(b)
        vop(prb, T.land[:, b * BLK:(b + 1) * BLK], T.gd[:, b * BLK:(b + 1) * BLK], AluOpType.mult)
        vsync()
        if i == 0:
            prev = prb
        else:
            out = T.s3[:] if i == len(order) - 1 else part[i % 2]
            vop(out, prb, prev, AluOpType.add)
            prev = out
    vsync()
    g.vector.tensor_tensor(T.yo[:], T.s3[:, 0:TOK], T.s3[:, TOK:BLK], AluOpType.add).then_inc(sem.yv, 1)
    g.sync.wait_ge(sem.yv, 1)
    g.sync.dma_start(T.y[:], T.yo[:]).then_inc(sem.stored, 16)
    g.sync.wait_ge(sem.stored, 16)
    g.wait_ge(sem.sent, sent[0])
